import numpy as np
import ml_dtypes


def mxq(x, axis, fmt="e4m3"):
    dtype, down = {"e4m3": (ml_dtypes.float8_e4m3fn, 7), "e5m2": (ml_dtypes.float8_e5m2, 14)}[fmt]
    v = np.moveaxis(np.asarray(x, np.float32).astype(ml_dtypes.bfloat16).astype(np.float64), axis, -1)
    blocks = v.reshape(v.shape[:-1] + (-1, 32))
    amax = np.abs(blocks).max(-1, keepdims=True)
    byte = np.maximum(np.where(amax > 0, np.frexp(amax)[1] - 1 + 127, 0) - down, 1)
    scale = np.exp2(byte - 127.0)
    codes = (blocks / scale).astype(np.float32).astype(dtype).astype(np.float64)
    return np.moveaxis((codes * scale).reshape(v.shape), -1, axis)


WIDE = False


def mx_kscale(k):
    if not WIDE:
        return np.ones(k)
    levels = np.array([30, -30])
    if k % 512:
        return np.exp2(np.random.permutation(np.resize(levels, k // 32))).repeat(32)
    a = np.empty((k // 512, 16))
    for p in range(k // 512):
        a[p, :8] = np.random.permutation(np.resize(levels, 8))
        for g in range(8):
            far = levels[np.abs(levels - a[p, g]) >= 10]
            a[p, g + 8] = far[np.random.randint(len(far))]
    return np.exp2(a.ravel()).repeat(32)


BF16 = ml_dtypes.bfloat16


def bf(x):
    return np.asarray(x, np.float32).astype(BF16)


def f64(x):
    return np.asarray(x).astype(np.float64)


E2M1 = np.array([0.0, 0.5, 1.0, 1.5, 2.0, 3.0, 4.0, 6.0, -0.0, -0.5, -1.0, -1.5, -2.0, -3.0, -4.0, -6.0])


def pack_weight(w, fmt):
    k, n = w.shape
    w = f64(bf(w)).reshape(k // 32, 32, n)
    amax = np.abs(w).max(1)
    if fmt in ("e4m3", "e5m2"):
        byte = np.frexp(amax)[1] - 1 + 127 - (7 if fmt == "e4m3" else 14)
    else:
        mant, ex = np.frexp(amax / 6.0)
        byte = np.where(mant > 0.5, ex, ex - 1) + 127
    byte = np.clip(np.where(amax > 0, byte, 1), 1, 254)
    scaled = (w * np.exp2(127.0 - byte)[:, None, :]).reshape(k, n).astype(np.float32)
    by_word = np.ascontiguousarray(scaled.reshape(k // 512, 128, 4, n).transpose(0, 1, 3, 2))
    if fmt in ("e4m3", "e5m2"):
        words = by_word.astype(ml_dtypes.float8_e4m3fn if fmt == "e4m3" else ml_dtypes.float8_e5m2).view(np.uint8)
    else:
        c = by_word.astype(ml_dtypes.float4_e2m1fn).view(np.uint8) & 0xF
        words = c[..., 0::2] | (c[..., 1::2] << 4)
    return np.ascontiguousarray(words), np.ascontiguousarray(byte.astype(np.uint8).reshape(k // 512, 16, n))


def unpack_weight(words, scales, fmt):
    g, p, n, _ = words.shape
    if fmt in ("e4m3", "e5m2"):
        vals = np.ascontiguousarray(words).view(ml_dtypes.float8_e4m3fn if fmt == "e4m3" else ml_dtypes.float8_e5m2).astype(np.float64)
    else:
        nib = np.empty((g, p, n, 4), np.uint8)
        nib[..., 0::2] = words & 0xF
        nib[..., 1::2] = words >> 4
        vals = E2M1[nib]
    vals = vals * np.repeat(np.exp2(scales.astype(np.float64) - 127.0), 8, axis=1)[..., None]
    return vals.transpose(0, 1, 3, 2).reshape(g * 512, n)


T, DK, DV = 2048, 512, 1024


def setup_inputs():
    s, t = mx_kscale(T), mx_kscale(DV)
    do = np.random.standard_normal((T, DV)) * np.exp(0.5 * np.random.standard_normal((T, DV)))
    g_words, g_scales = pack_weight(do * s[:, None], "e5m2")
    h_words, h_scales = pack_weight((do * t).T, "e5m2")
    gate = 0.5 + 0.5 * np.random.random((T, DK))
    qg = np.random.standard_normal((T, DK)) * gate / np.sqrt(T)
    return {"g_words": g_words, "g_scales": g_scales,
            "h_words": h_words, "h_scales": h_scales,
            "qg": bf(qg / s[:, None]),
            "state": bf(np.random.standard_normal((DK, DV)) / np.sqrt(DV) / t),
            "gate": bf(gate),
            "dq_rest": bf(np.random.standard_normal((T, DK))),
            "decay": bf(0.5 + 0.5 * np.random.random(DK)),
            "ds_next": bf(np.random.standard_normal((DK, DV)))}


def reference(g_words, g_scales, h_words, h_scales, qg, state, gate, dq_rest, decay, ds_next):
    g = unpack_weight(g_words, g_scales, "e5m2")
    h = unpack_weight(h_words, h_scales, "e5m2")
    read = h.T @ mxq(f64(state), 1, "e4m3").T
    dq = f64(gate) * read + f64(dq_rest)
    outer = mxq(f64(qg), 0, "e4m3").T @ g
    ds = outer + f64(decay)[:, None] * f64(ds_next)
    return dq, ds

@@ -1,0 +1,216 @@
+from contextlib import ExitStack
+
+import concourse.mybir as mybir
+from concourse.masks import make_identity
+
+T, DK, DV = 2048, 512, 1024
+FLOPS = 2 * 2 * T * DK * DV
+
+F32 = mybir.dt.float32
+BF16 = mybir.dt.bfloat16
+U32 = mybir.dt.uint32
+I32 = mybir.dt.int32
+U8 = mybir.dt.uint8
+E4M3X4 = mybir.dt.float8_e4m3fn_x4
+E5M2X4 = mybir.dt.float8_e5m2_x4
+ADD = mybir.AluOpType.add
+MULT = mybir.AluOpType.mult
+
+P = 128
+K_PASS = 512
+N_BANK = 512
+T_PASSES = T // K_PASS
+V_PASSES = DV // K_PASS
+DK_TILES = DK // P
+TOK_TILES = T // P
+CHUNKS = [4, 4, 4, 2, 1, 1]
+
+
+def tile_linear_attention_state_backward_e2_kernel(
+    tc, g_words, g_scales, h_words, h_scales, qg, state, gate, dq_rest, decay, ds_next, dq_out, ds_out
+):
+    nc = tc.nc
+    with ExitStack() as ctx:
+        keep = ctx.enter_context(tc.tile_pool(name="keep", bufs=1))
+        outs = ctx.enter_context(tc.tile_pool(name="outs", bufs=6))
+        psum = ctx.enter_context(tc.psum_pool(name="psum", bufs=8))
+        ctx.enter_context(tc.manual_schedule())
+
+        ident = keep.tile([P, P], F32, name="ident")
+        make_identity(nc, ident[:])
+
+        g_sc = keep.tile([P, T_PASSES, DV], U8, align_bytes=64, name="g_sc")
+        h_sc = keep.tile([P, V_PASSES, T], U8, align_bytes=64, name="h_sc")
+        nc.vector.memset(g_sc[:].rearrange("p g n -> p (g n)").bitcast(I32), 0)
+        nc.vector.memset(h_sc[:].rearrange("p g n -> p (g n)").bitcast(I32), 0)
+
+        qg_raw = [keep.tile([P, 4, DK], BF16, name="qg_raw%d" % c) for c in range(T_PASSES)]
+
+        def load_qg(c):
+            nc.sync.dma_start(
+                out=qg_raw[c][:],
+                in_=qg[c * K_PASS : (c + 1) * K_PASS, :].rearrange("(p j) w -> p j w", j=4),
+            )
+
+        def load_scales(tile, hbm):
+            rows = hbm.rearrange("g q n -> q g n").bitcast(I32)
+            for q in range(4):
+                nc.sync.dma_start(
+                    out=tile[32 * q : 32 * q + 4, :, :].bitcast(I32),
+                    in_=rows[4 * q : 4 * q + 4, :, :],
+                )
+
+        load_qg(0)
+        load_qg(1)
+        load_scales(g_sc, g_scales)
+        load_qg(2)
+        load_qg(3)
+
+        st_raw = keep.tile([P, DK_TILES, DV], BF16, name="st_raw")
+        st_view = state.rearrange("(i p) v -> p i v", p=P)
+        for i in range(0, DK_TILES, 2):
+            nc.sync.dma_start(out=st_raw[:, i : i + 2, :], in_=st_view[:, i : i + 2, :])
+
+        g_w = []
+        for c in range(T_PASSES):
+            w = keep.tile([P, DV], U32, align_bytes=64, name="g_w%d" % c)
+            nc.sync.dma_start(out=w[:].bitcast(I32), in_=g_words[c].rearrange("p n t -> p (n t)").bitcast(I32))
+            g_w.append(w)
+
+        dsn = keep.tile([P, DK_TILES, DV], BF16, name="dsn")
+        nc.sync.dma_start(out=dsn[:], in_=ds_next.rearrange("(i p) v -> p i v", p=P))
+        dec_b = keep.tile([P, DK_TILES], BF16, name="dec_b")
+        with nc.allow_non_contiguous_dma(reason="512 small values"):
+            nc.sync.dma_start(out=dec_b[:], in_=decay.rearrange("(i p) -> p i", p=P))
+        load_scales(h_sc, h_scales)
+
+        h_w = [keep.tile([P, V_PASSES, T // 2], U32, align_bytes=64, name="h_w%d" % b) for b in range(2)]
+        h_view = h_words.rearrange("g p n t -> p g (n t)").bitcast(I32)
+
+        def load_h(b):
+            nc.sync.dma_start(
+                out=h_w[b][:].bitcast(I32), in_=h_view[:, :, b * (T // 2) : (b + 1) * (T // 2)]
+            )
+
+        gate_t = keep.tile([P, TOK_TILES, DK], BF16, name="gate_t")
+        rest_t = keep.tile([P, TOK_TILES, DK], BF16, name="rest_t")
+        gate_view = gate.rearrange("(i p) k -> p i k", p=P)
+        rest_view = dq_rest.rearrange("(i p) k -> p i k", p=P)
+
+        def load_chunk(i0, n):
+            nc.sync.dma_start(out=gate_t[:, i0 : i0 + n, :], in_=gate_view[:, i0 : i0 + n, :])
+            nc.sync.dma_start(out=rest_t[:, i0 : i0 + n, :], in_=rest_view[:, i0 : i0 + n, :])
+
+        i0 = 0
+        for n in CHUNKS:
+            if i0 == 0:
+                load_h(0)
+            if i0 == TOK_TILES // 2:
+                load_h(1)
+            load_chunk(i0, n)
+            i0 += n
+
+        qg_grp = [keep.tile([P, DK, 4], BF16, align_bytes=64, name="qg_grp%d" % c) for c in range(T_PASSES)]
+        qg_c = [keep.tile([P, DK], U32, align_bytes=64, name="qg_c%d" % c) for c in range(T_PASSES)]
+        qg_s = [keep.tile([P, DK], U8, align_bytes=64, name="qg_s%d" % c) for c in range(T_PASSES)]
+        st_grp = [keep.tile([P, DK, 4], BF16, align_bytes=64, name="st_grp%d" % c) for c in range(V_PASSES)]
+        st_c = [keep.tile([P, DK], U32, align_bytes=64, name="st_c%d" % c) for c in range(V_PASSES)]
+        st_s = [keep.tile([P, DK], U8, align_bytes=64, name="st_s%d" % c) for c in range(V_PASSES)]
+
+        def interleave(c, on_vector):
+            src = qg_raw[c][:].rearrange("p j w -> p w j")
+            if on_vector:
+                nc.vector.tensor_copy(out=qg_grp[c][:], in_=src)
+            else:
+                nc.scalar.copy(out=qg_grp[c][:], in_=src)
+
+        def quantize(codes, scales, grouped):
+            nc.vector.quantize_mx(
+                out=codes[:].bitcast(E4M3X4), scales=scales[:], in_=grouped[:].rearrange("p w j -> p (w j)")
+            )
+
+        words = st_raw[:].rearrange("p i v -> p (i v)").bitcast(F32)
+
+        def transpose_state(c, half):
+            bank = psum.tile([P, 2, 2 * P], F32, name="bank", tag="bank")
+            for i in range(2):
+                for u in range(2):
+                    w0 = (2 * half + i) * (DV // 2) + c * (K_PASS // 2) + u
+                    nc.tensor.transpose(
+                        bank[:, u, i * P : (i + 1) * P], words[:, w0 : w0 + 2 * P - 1 : 2], ident[:]
+                    )
+            nc.scalar.copy(
+                out=st_grp[c][:, half * 2 * P : (half + 1) * 2 * P, :].rearrange("p r t -> p (r t)").bitcast(F32).rearrange("p (r u) -> p r u", u=2),
+                in_=bank[:].rearrange("p u r -> p r u"),
+            )
+
+        interleave(0, True)
+        interleave(1, False)
+        quantize(qg_c[0], qg_s[0], qg_grp[0])
+        interleave(2, True)
+        quantize(qg_c[1], qg_s[1], qg_grp[1])
+        interleave(3, False)
+        quantize(qg_c[2], qg_s[2], qg_grp[2])
+        quantize(qg_c[3], qg_s[3], qg_grp[3])
+        for half in range(2):
+            for c in range(V_PASSES):
+                transpose_state(c, half)
+        for c in range(V_PASSES):
+            quantize(st_c[c], st_s[c], st_grp[c])
+        dec = keep.tile([P, DK_TILES], F32, name="dec")
+        nc.scalar.copy(out=dec[:], in_=dec_b[:])
+
+        acc = [[psum.tile([P, N_BANK], F32, name="bank", tag="bank") for h in range(2)] for t in range(DK_TILES)]
+        for c in range(T_PASSES):
+            for t in range(DK_TILES):
+                for h in range(2):
+                    ms = slice(t * P, (t + 1) * P)
+                    ns = slice(h * N_BANK, (h + 1) * N_BANK)
+                    nc.tensor.matmul_mx(
+                        out=acc[t][h][:],
+                        lhsT=qg_c[c][:, ms].bitcast(E4M3X4),
+                        lhsT_scale=qg_s[c][:, ms],
+                        rhs=g_w[c][:, ns].bitcast(E5M2X4),
+                        rhs_scale=g_sc[:, c, ns],
+                        start=(c == 0),
+                        stop=(c == T_PASSES - 1),
+                    )
+        for t in range(DK_TILES):
+            ds_sb = keep.tile([P, DV], F32, name="ds_sb%d" % t)
+            for h in range(2):
+                ns = slice(h * N_BANK, (h + 1) * N_BANK)
+                nc.vector.scalar_tensor_tensor(
+                    out=ds_sb[:, ns], in0=dsn[:, t, ns], scalar=dec[:, t : t + 1], in1=acc[t][h][:], op0=MULT, op1=ADD
+                )
+            nc.gpsimd.dma_start(out=ds_out[t * P : (t + 1) * P, :], in_=ds_sb[:])
+
+        prods = {}
+
+        def matmul_tok(i):
+            bank = psum.tile([P, DK], F32, name="bank", tag="bank")
+            b, r = divmod(i * P, T // 2)
+            for c in range(V_PASSES):
+                nc.tensor.matmul_mx(
+                    out=bank[:],
+                    lhsT=h_w[b][:, c, r : r + P].bitcast(E5M2X4),
+                    lhsT_scale=h_sc[:, c, i * P : (i + 1) * P],
+                    rhs=st_c[c][:].bitcast(E4M3X4),
+                    rhs_scale=st_s[c][:],
+                    start=(c == 0),
+                    stop=(c == V_PASSES - 1),
+                )
+            prod = outs.tile([P, DK], F32, name="prod")
+            nc.vector.tensor_tensor(out=prod[:], in0=bank[:], in1=gate_t[:, i, :], op=MULT)
+            prods[i] = prod
+
+        def finish_tok(i):
+            dq_sb = outs.tile([P, DK], F32, name="dq_sb")
+            nc.vector.tensor_tensor(out=dq_sb[:], in0=prods[i][:], in1=rest_t[:, i, :], op=ADD)
+            eng = nc.gpsimd if i < TOK_TILES - 3 else nc.sync
+            eng.dma_start(out=dq_out[i * P : (i + 1) * P, :], in_=dq_sb[:])
+
+        for i in range(TOK_TILES):
+            matmul_tok(i)
+            if i > 0:
+                finish_tok(i - 1)
+        finish_tok(TOK_TILES - 1)

@@ -23,7 +23,10 @@ T_PASSES = T // K_PASS
 V_PASSES = DV // K_PASS
 DK_TILES = DK // P
 TOK_TILES = T // P
-CHUNKS = [4, 4, 4, 2, 1, 1]
+
+I_TOK = 4
+BLOCK = P * I_TOK
+BLOCKS = T // BLOCK
 
 
 def tile_linear_attention_state_backward_e2_kernel(
@@ -32,8 +35,8 @@ def tile_linear_attention_state_backward_e2_kernel(
     nc = tc.nc
     with ExitStack() as ctx:
         keep = ctx.enter_context(tc.tile_pool(name="keep", bufs=1))
-        outs = ctx.enter_context(tc.tile_pool(name="outs", bufs=6))
-        psum = ctx.enter_context(tc.psum_pool(name="psum", bufs=8))
+        outs = ctx.enter_context(tc.tile_pool(name="outs", bufs=4))
+        psum = ctx.enter_context(tc.psum_pool(name="psum", bufs=4))
         ctx.enter_context(tc.manual_schedule())
 
         ident = keep.tile([P, P], F32, name="ident")
@@ -41,16 +44,8 @@ def tile_linear_attention_state_backward_e2_kernel(
 
         g_sc = keep.tile([P, T_PASSES, DV], U8, align_bytes=64, name="g_sc")
         h_sc = keep.tile([P, V_PASSES, T], U8, align_bytes=64, name="h_sc")
-        nc.vector.memset(g_sc[:].rearrange("p g n -> p (g n)").bitcast(I32), 0)
         nc.vector.memset(h_sc[:].rearrange("p g n -> p (g n)").bitcast(I32), 0)
-
-        qg_raw = [keep.tile([P, 4, DK], BF16, name="qg_raw%d" % c) for c in range(T_PASSES)]
-
-        def load_qg(c):
-            nc.sync.dma_start(
-                out=qg_raw[c][:],
-                in_=qg[c * K_PASS : (c + 1) * K_PASS, :].rearrange("(p j) w -> p j w", j=4),
-            )
+        nc.vector.memset(g_sc[:].rearrange("p g n -> p (g n)").bitcast(I32), 0)
 
         def load_scales(tile, hbm):
             rows = hbm.rearrange("g q n -> q g n").bitcast(I32)
@@ -60,29 +55,12 @@ def tile_linear_attention_state_backward_e2_kernel(
                     in_=rows[4 * q : 4 * q + 4, :, :],
                 )
 
-        load_qg(0)
-        load_qg(1)
-        load_scales(g_sc, g_scales)
-        load_qg(2)
-        load_qg(3)
 
-        st_raw = keep.tile([P, DK_TILES, DV], BF16, name="st_raw")
-        st_view = state.rearrange("(i p) v -> p i v", p=P)
-        for i in range(0, DK_TILES, 2):
-            nc.sync.dma_start(out=st_raw[:, i : i + 2, :], in_=st_view[:, i : i + 2, :])
+        st_raw = keep.tile([P, 4, DV], BF16, name="st_raw")
+        st_view = state.rearrange("(r i) v -> r i v", i=4)
 
-        g_w = []
-        for c in range(T_PASSES):
-            w = keep.tile([P, DV], U32, align_bytes=64, name="g_w%d" % c)
-            nc.sync.dma_start(out=w[:].bitcast(I32), in_=g_words[c].rearrange("p n t -> p (n t)").bitcast(I32))
-            g_w.append(w)
-
-        dsn = keep.tile([P, DK_TILES, DV], BF16, name="dsn")
-        nc.sync.dma_start(out=dsn[:], in_=ds_next.rearrange("(i p) v -> p i v", p=P))
-        dec_b = keep.tile([P, DK_TILES], BF16, name="dec_b")
-        with nc.allow_non_contiguous_dma(reason="512 small values"):
-            nc.sync.dma_start(out=dec_b[:], in_=decay.rearrange("(i p) -> p i", p=P))
-        load_scales(h_sc, h_scales)
+        def load_state(a):
+            nc.sync.dma_start(out=st_raw[:, 2 * a : 2 * a + 2, :], in_=st_view[:, 2 * a : 2 * a + 2, :])
 
         h_w = [keep.tile([P, V_PASSES, T // 2], U32, align_bytes=64, name="h_w%d" % b) for b in range(2)]
         h_view = h_words.rearrange("g p n t -> p g (n t)").bitcast(I32)
@@ -92,23 +70,52 @@ def tile_linear_attention_state_backward_e2_kernel(
                 out=h_w[b][:].bitcast(I32), in_=h_view[:, :, b * (T // 2) : (b + 1) * (T // 2)]
             )
 
-        gate_t = keep.tile([P, TOK_TILES, DK], BF16, name="gate_t")
-        rest_t = keep.tile([P, TOK_TILES, DK], BF16, name="rest_t")
-        gate_view = gate.rearrange("(i p) k -> p i k", p=P)
-        rest_view = dq_rest.rearrange("(i p) k -> p i k", p=P)
+        gate_t = [keep.tile([P, I_TOK, DK], BF16, name="gate%d" % b) for b in range(BLOCKS)]
+        rest_t = [keep.tile([P, I_TOK, DK], BF16, name="rest%d" % b) for b in range(BLOCKS)]
+        gate_view = gate.rearrange("(b m i) k -> b m i k", m=P, i=I_TOK)
+        rest_view = dq_rest.rearrange("(b m i) k -> b m i k", m=P, i=I_TOK)
+        dq_view = dq_out.rearrange("(b m i) k -> b m i k", m=P, i=I_TOK)
 
-        def load_chunk(i0, n):
-            nc.sync.dma_start(out=gate_t[:, i0 : i0 + n, :], in_=gate_view[:, i0 : i0 + n, :])
-            nc.sync.dma_start(out=rest_t[:, i0 : i0 + n, :], in_=rest_view[:, i0 : i0 + n, :])
+        def load_block(b):
+            nc.sync.dma_start(out=gate_t[b][:], in_=gate_view[b])
+            nc.sync.dma_start(out=rest_t[b][:], in_=rest_view[b])
 
-        i0 = 0
-        for n in CHUNKS:
-            if i0 == 0:
-                load_h(0)
-            if i0 == TOK_TILES // 2:
-                load_h(1)
-            load_chunk(i0, n)
-            i0 += n
+        qg_raw = [keep.tile([P, 4, DK], BF16, name="qg_raw%d" % c) for c in range(T_PASSES)]
+
+        def load_qg(c):
+            nc.sync.dma_start(
+                out=qg_raw[c][:],
+                in_=qg[c * K_PASS : (c + 1) * K_PASS, :].rearrange("(p j) w -> p j w", j=4),
+            )
+
+        g_w = [keep.tile([P, DV], U32, align_bytes=64, name="g_w%d" % c) for c in range(T_PASSES)]
+
+        def load_g(c):
+            nc.sync.dma_start(
+                out=g_w[c][:].bitcast(I32), in_=g_words[c].rearrange("p n t -> p (n t)").bitcast(I32)
+            )
+
+        dsn = keep.tile([P, DK_TILES, DV], BF16, name="dsn")
+
+        load_state(0)
+        load_state(1)
+        load_scales(h_sc, h_scales)
+        load_h(0)
+        load_block(0)
+        load_qg(0)
+        load_qg(1)
+        load_block(1)
+        load_scales(g_sc, g_scales)
+        load_qg(2)
+        load_qg(3)
+        load_h(1)
+        load_block(2)
+        for c in range(T_PASSES):
+            load_g(c)
+        nc.sync.dma_start(out=dsn[:], in_=ds_next.rearrange("(m t) v -> m t v", t=DK_TILES))
+        dec_b = keep.tile([P, DK_TILES], BF16, name="dec_b")
+        nc.sync.dma_start(out=dec_b[:], in_=decay.rearrange("(m t) -> m t", t=DK_TILES))
+        load_block(3)
 
         qg_grp = [keep.tile([P, DK, 4], BF16, align_bytes=64, name="qg_grp%d" % c) for c in range(T_PASSES)]
         qg_c = [keep.tile([P, DK], U32, align_bytes=64, name="qg_c%d" % c) for c in range(T_PASSES)]
@@ -116,13 +123,6 @@ def tile_linear_attention_state_backward_e2_kernel(
         st_grp = [keep.tile([P, DK, 4], BF16, align_bytes=64, name="st_grp%d" % c) for c in range(V_PASSES)]
         st_c = [keep.tile([P, DK], U32, align_bytes=64, name="st_c%d" % c) for c in range(V_PASSES)]
         st_s = [keep.tile([P, DK], U8, align_bytes=64, name="st_s%d" % c) for c in range(V_PASSES)]
-
-        def interleave(c, on_vector):
-            src = qg_raw[c][:].rearrange("p j w -> p w j")
-            if on_vector:
-                nc.vector.tensor_copy(out=qg_grp[c][:], in_=src)
-            else:
-                nc.scalar.copy(out=qg_grp[c][:], in_=src)
 
         def quantize(codes, scales, grouped):
             nc.vector.quantize_mx(
@@ -132,42 +132,92 @@ def tile_linear_attention_state_backward_e2_kernel(
         words = st_raw[:].rearrange("p i v -> p (i v)").bitcast(F32)
 
         def transpose_state(c, half):
-            bank = psum.tile([P, 2, 2 * P], F32, name="bank", tag="bank")
+            bank = psum.tile([P, 2, 2, P], F32, name="bank", tag="bank")
             for i in range(2):
                 for u in range(2):
                     w0 = (2 * half + i) * (DV // 2) + c * (K_PASS // 2) + u
-                    nc.tensor.transpose(
-                        bank[:, u, i * P : (i + 1) * P], words[:, w0 : w0 + 2 * P - 1 : 2], ident[:]
-                    )
-            nc.scalar.copy(
-                out=st_grp[c][:, half * 2 * P : (half + 1) * 2 * P, :].rearrange("p r t -> p (r t)").bitcast(F32).rearrange("p (r u) -> p r u", u=2),
-                in_=bank[:].rearrange("p u r -> p r u"),
-            )
+                    nc.tensor.transpose(bank[:, u, i, :], words[:, w0 : w0 + 2 * P - 1 : 2], ident[:])
+            dst = st_grp[c][:].rearrange("p w t -> p (w t)").bitcast(F32)
+            dst = dst.rearrange("p (r i u) -> p r i u", i=4, u=2)[:, :, 2 * half : 2 * half + 2, :]
+            nc.scalar.copy(out=dst, in_=bank[:].rearrange("p u i r -> p r i u"))
 
-        interleave(0, True)
-        interleave(1, False)
-        quantize(qg_c[0], qg_s[0], qg_grp[0])
-        interleave(2, True)
-        quantize(qg_c[1], qg_s[1], qg_grp[1])
-        interleave(3, False)
-        quantize(qg_c[2], qg_s[2], qg_grp[2])
-        quantize(qg_c[3], qg_s[3], qg_grp[3])
         for half in range(2):
             for c in range(V_PASSES):
                 transpose_state(c, half)
         for c in range(V_PASSES):
             quantize(st_c[c], st_s[c], st_grp[c])
-        dec = keep.tile([P, DK_TILES], F32, name="dec")
-        nc.scalar.copy(out=dec[:], in_=dec_b[:])
 
-        acc = [[psum.tile([P, N_BANK], F32, name="bank", tag="bank") for h in range(2)] for t in range(DK_TILES)]
-        for c in range(T_PASSES):
-            for t in range(DK_TILES):
+        h_p = [keep.tile([P, V_PASSES, BLOCK], U32, align_bytes=64, name="h_p%d" % b) for b in range(BLOCKS)]
+        h_ps = [keep.tile([P, V_PASSES, BLOCK], U8, align_bytes=64, name="h_ps%d" % b) for b in range(BLOCKS)]
+
+        def permute(b):
+            half, r = divmod(b * BLOCK, T // 2)
+            for c in range(V_PASSES):
+                nc.vector.tensor_copy(
+                    out=h_p[b][:, c, :].bitcast(I32).rearrange("p (i mb mi) -> p mb i mi", i=I_TOK, mi=4),
+                    in_=h_w[half][:, c, r : r + BLOCK].bitcast(I32).rearrange("p (mb mi i) -> p mb i mi", i=I_TOK, mi=4),
+                )
+                nc.vector.tensor_copy(
+                    out=h_ps[b][:, c, :].rearrange("p (i mb mi) -> p mb i mi", i=I_TOK, mi=16),
+                    in_=h_sc[:, c, b * BLOCK : (b + 1) * BLOCK].rearrange("p (mb mi i) -> p mb i mi", i=I_TOK, mi=16),
+                )
+
+        pending = []
+
+        dq_sb = [keep.tile([P, I_TOK, DK], F32, name="dq_sb%d" % b) for b in range(BLOCKS)]
+
+        def finish_pair():
+            b, a, prod = pending.pop(0)
+            toks = slice(2 * a, 2 * a + 2)
+            nc.vector.tensor_tensor(out=dq_sb[b][:, toks, :], in0=prod[:], in1=rest_t[b][:, toks, :], op=ADD)
+            if b == BLOCKS - 1:
+                nc.sync.dma_start(out=dq_view[b, :, toks, :], in_=dq_sb[b][:, toks, :])
+            elif a == 1:
+                nc.sync.dma_start(out=dq_view[b], in_=dq_sb[b][:])
+
+        banks = {}
+
+        def queries_matmul(b, i):
+            bank = psum.tile([P, DK], F32, name="bank", tag="bank")
+            for c in range(V_PASSES):
+                nc.tensor.matmul_mx(
+                    out=bank[:],
+                    lhsT=h_p[b][:, c, i * P : (i + 1) * P].bitcast(E5M2X4),
+                    lhsT_scale=h_ps[b][:, c, i * P : (i + 1) * P],
+                    rhs=st_c[c][:].bitcast(E4M3X4),
+                    rhs_scale=st_s[c][:],
+                    start=(c == 0),
+                    stop=(c == V_PASSES - 1),
+                )
+            banks[b, i] = bank
+
+        def queries_gate(b, a):
+            prod = outs.tile([P, 2, DK], F32, name="prod")
+            for j in range(2):
+                i = 2 * a + j
+                nc.vector.tensor_tensor(out=prod[:, j, :], in0=banks[b, i][:], in1=gate_t[b][:, i, :], op=MULT)
+            if pending:
+                finish_pair()
+            pending.append((b, a, prod))
+
+        def queries_block(b):
+            for a in range(2):
+                for j in range(2):
+                    queries_matmul(b, 2 * a + j)
+                queries_gate(b, a)
+
+        acc = {}
+        ds_view = ds_out.rearrange("(m t) v -> m t v", t=DK_TILES)
+
+        def state_pass(a, c):
+            for t in (2 * a, 2 * a + 1):
                 for h in range(2):
+                    if c == 0:
+                        acc[t, h] = psum.tile([P, N_BANK], F32, name="acc", tag="acc")
                     ms = slice(t * P, (t + 1) * P)
                     ns = slice(h * N_BANK, (h + 1) * N_BANK)
                     nc.tensor.matmul_mx(
-                        out=acc[t][h][:],
+                        out=acc[t, h][:],
                         lhsT=qg_c[c][:, ms].bitcast(E4M3X4),
                         lhsT_scale=qg_s[c][:, ms],
                         rhs=g_w[c][:, ns].bitcast(E5M2X4),
@@ -175,42 +225,48 @@ def tile_linear_attention_state_backward_e2_kernel(
                         start=(c == 0),
                         stop=(c == T_PASSES - 1),
                     )
-        for t in range(DK_TILES):
-            ds_sb = keep.tile([P, DV], F32, name="ds_sb%d" % t)
-            for h in range(2):
-                ns = slice(h * N_BANK, (h + 1) * N_BANK)
-                nc.vector.scalar_tensor_tensor(
-                    out=ds_sb[:, ns], in0=dsn[:, t, ns], scalar=dec[:, t : t + 1], in1=acc[t][h][:], op0=MULT, op1=ADD
-                )
-            nc.gpsimd.dma_start(out=ds_out[t * P : (t + 1) * P, :], in_=ds_sb[:])
 
-        prods = {}
+        def state_finish(a):
+            ds_sb = keep.tile([P, 2, DV], F32, name="ds_sb%d" % a)
+            for t in (2 * a, 2 * a + 1):
+                for h in range(2):
+                    ns = slice(h * N_BANK, (h + 1) * N_BANK)
+                    nc.vector.scalar_tensor_tensor(
+                        out=ds_sb[:, t - 2 * a, ns],
+                        in0=dsn[:, t, ns],
+                        scalar=dec[:, t : t + 1],
+                        in1=acc[t, h][:],
+                        op0=MULT,
+                        op1=ADD,
+                    )
+            nc.sync.dma_start(out=ds_view[:, 2 * a : 2 * a + 2, :], in_=ds_sb[:])
 
-        def matmul_tok(i):
-            bank = psum.tile([P, DK], F32, name="bank", tag="bank")
-            b, r = divmod(i * P, T // 2)
-            for c in range(V_PASSES):
-                nc.tensor.matmul_mx(
-                    out=bank[:],
-                    lhsT=h_w[b][:, c, r : r + P].bitcast(E5M2X4),
-                    lhsT_scale=h_sc[:, c, i * P : (i + 1) * P],
-                    rhs=st_c[c][:].bitcast(E4M3X4),
-                    rhs_scale=st_s[c][:],
-                    start=(c == 0),
-                    stop=(c == V_PASSES - 1),
-                )
-            prod = outs.tile([P, DK], F32, name="prod")
-            nc.vector.tensor_tensor(out=prod[:], in0=bank[:], in1=gate_t[:, i, :], op=MULT)
-            prods[i] = prod
+        for c in range(T_PASSES):
+            nc.scalar.copy(
+                out=qg_grp[c][:].rearrange("p (t m) j -> p t m j", t=DK_TILES),
+                in_=qg_raw[c][:].rearrange("p j (m t) -> p t m j", t=DK_TILES),
+            )
+        dec = keep.tile([P, DK_TILES], F32, name="dec")
+        nc.scalar.copy(out=dec[:], in_=dec_b[:])
 
-        def finish_tok(i):
-            dq_sb = outs.tile([P, DK], F32, name="dq_sb")
-            nc.vector.tensor_tensor(out=dq_sb[:], in0=prods[i][:], in1=rest_t[:, i, :], op=ADD)
-            eng = nc.gpsimd if i < TOK_TILES - 3 else nc.sync
-            eng.dma_start(out=dq_out[i * P : (i + 1) * P, :], in_=dq_sb[:])
-
-        for i in range(TOK_TILES):
-            matmul_tok(i)
-            if i > 0:
-                finish_tok(i - 1)
-        finish_tok(TOK_TILES - 1)
+        permute(0)
+        permute(1)
+        queries_block(0)
+        queries_block(1)
+        finish_pair()
+        for c in range(T_PASSES):
+            quantize(qg_c[c], qg_s[c], qg_grp[c])
+        permute(2)
+        permute(3)
+        for i in range(I_TOK):
+            queries_matmul(2, i)
+            state_pass(0, i)
+        queries_gate(2, 0)
+        queries_gate(2, 1)
+        finish_pair()
+        state_finish(0)
+        queries_block(3)
+        finish_pair()
+        for c in range(T_PASSES):
+            state_pass(1, c)
+        state_finish(1)

@@ -76,10 +76,6 @@ def tile_linear_attention_state_backward_e2_kernel(
         rest_view = dq_rest.rearrange("(b m i) k -> b m i k", m=P, i=I_TOK)
         dq_view = dq_out.rearrange("(b m i) k -> b m i k", m=P, i=I_TOK)
 
-        def load_block(b):
-            nc.sync.dma_start(out=gate_t[b][:], in_=gate_view[b])
-            nc.sync.dma_start(out=rest_t[b][:], in_=rest_view[b])
-
         qg_raw = [keep.tile([P, 4, DK], BF16, name="qg_raw%d" % c) for c in range(T_PASSES)]
 
         def load_qg(c):
@@ -97,25 +93,36 @@ def tile_linear_attention_state_backward_e2_kernel(
 
         dsn = keep.tile([P, DK_TILES, DV], BF16, name="dsn")
 
+        def load_gate(b):
+            nc.sync.dma_start(out=gate_t[b][:], in_=gate_view[b])
+
+        def load_rest(b):
+            nc.sync.dma_start(out=rest_t[b][:], in_=rest_view[b])
+
+        dec_b = keep.tile([P, DK_TILES], BF16, name="dec_b")
+
         load_state(0)
         load_state(1)
         load_scales(h_sc, h_scales)
         load_h(0)
-        load_block(0)
+        load_gate(0)
         load_qg(0)
+        load_rest(0)
         load_qg(1)
-        load_block(1)
-        load_scales(g_sc, g_scales)
+        load_gate(1)
         load_qg(2)
+        load_rest(1)
         load_qg(3)
-        load_h(1)
-        load_block(2)
+        load_scales(g_sc, g_scales)
+        nc.sync.dma_start(out=dec_b[:], in_=decay.rearrange("(m t) -> m t", t=DK_TILES))
         for c in range(T_PASSES):
             load_g(c)
+        load_h(1)
         nc.sync.dma_start(out=dsn[:], in_=ds_next.rearrange("(m t) v -> m t v", t=DK_TILES))
-        dec_b = keep.tile([P, DK_TILES], BF16, name="dec_b")
-        nc.sync.dma_start(out=dec_b[:], in_=decay.rearrange("(m t) -> m t", t=DK_TILES))
-        load_block(3)
+        load_gate(2)
+        load_rest(2)
+        load_gate(3)
+        load_rest(3)
 
         qg_grp = [keep.tile([P, DK, 4], BF16, align_bytes=64, name="qg_grp%d" % c) for c in range(T_PASSES)]
         qg_c = [keep.tile([P, DK], U32, align_bytes=64, name="qg_c%d" % c) for c in range(T_PASSES)]
@@ -169,7 +176,8 @@ def tile_linear_attention_state_backward_e2_kernel(
         def finish_pair():
             b, a, prod = pending.pop(0)
             toks = slice(2 * a, 2 * a + 2)
-            nc.vector.tensor_tensor(out=dq_sb[b][:, toks, :], in0=prod[:], in1=rest_t[b][:, toks, :], op=ADD)
+            eng = nc.vector if b < 2 else nc.gpsimd
+            eng.tensor_tensor(out=dq_sb[b][:, toks, :], in0=prod[:], in1=rest_t[b][:, toks, :], op=ADD)
             if b == BLOCKS - 1:
                 nc.sync.dma_start(out=dq_view[b, :, toks, :], in_=dq_sb[b][:, toks, :])
             elif a == 1:
@@ -243,8 +251,8 @@ def tile_linear_attention_state_backward_e2_kernel(
 
         for c in range(T_PASSES):
             nc.scalar.copy(
-                out=qg_grp[c][:].rearrange("p (t m) j -> p t m j", t=DK_TILES),
-                in_=qg_raw[c][:].rearrange("p j (m t) -> p t m j", t=DK_TILES),
+                out=qg_grp[c][:].rearrange("p (t m) j -> p m t j", t=DK_TILES),
+                in_=qg_raw[c][:].rearrange("p j (m t) -> p m t j", t=DK_TILES),
             )
         dec = keep.tile([P, DK_TILES], F32, name="dec")
         nc.scalar.copy(out=dec[:], in_=dec_b[:])
@@ -258,15 +266,17 @@ def tile_linear_attention_state_backward_e2_kernel(
             quantize(qg_c[c], qg_s[c], qg_grp[c])
         permute(2)
         permute(3)
+        for c in range(T_PASSES):
+            state_pass(0, c)
+        state_finish(0)
         for i in range(I_TOK):
             queries_matmul(2, i)
-            state_pass(0, i)
         queries_gate(2, 0)
         queries_gate(2, 1)
+        for i in range(I_TOK):
+            state_pass(1, i)
+            queries_matmul(3, i)
+        queries_gate(3, 0)
+        queries_gate(3, 1)
         finish_pair()
-        state_finish(0)
-        queries_block(3)
-        finish_pair()
-        for c in range(T_PASSES):
-            state_pass(1, c)
         state_finish(1)

@@ -48,12 +48,9 @@ def tile_linear_attention_state_backward_e2_kernel(
         nc.vector.memset(g_sc[:].rearrange("p g n -> p (g n)").bitcast(I32), 0)
 
         def load_scales(tile, hbm):
-            rows = hbm.rearrange("g q n -> q g n").bitcast(I32)
-            for q in range(4):
-                nc.sync.dma_start(
-                    out=tile[32 * q : 32 * q + 4, :, :].bitcast(I32),
-                    in_=rows[4 * q : 4 * q + 4, :, :],
-                )
+            rows = hbm.rearrange("g (q r) n -> r q g n", r=4).bitcast(I32)
+            for r in range(4):
+                nc.sync.dma_start(out=tile[r : P : 32, :, :].bitcast(I32), in_=rows[r])
 
 
         st_raw = keep.tile([P, 4, DV], BF16, name="st_raw")

@@ -244,7 +244,7 @@ def tile_linear_attention_state_backward_e2_kernel(
                         op0=MULT,
                         op1=ADD,
                     )
-            nc.sync.dma_start(out=ds_view[:, 2 * a : 2 * a + 2, :], in_=ds_sb[:])
+            nc.scalar.dma_start(out=ds_view[:, 2 * a : 2 * a + 2, :], in_=ds_sb[:])
 
         for c in range(T_PASSES):
             nc.scalar.copy(

from contextlib import ExitStack

import concourse.mybir as mybir
from concourse.masks import make_identity

T, DK, DV = 2048, 512, 1024
FLOPS = 2 * 2 * T * DK * DV

F32 = mybir.dt.float32
BF16 = mybir.dt.bfloat16
U32 = mybir.dt.uint32
I32 = mybir.dt.int32
U8 = mybir.dt.uint8
E4M3X4 = mybir.dt.float8_e4m3fn_x4
E5M2X4 = mybir.dt.float8_e5m2_x4
ADD = mybir.AluOpType.add
MULT = mybir.AluOpType.mult

P = 128
K_PASS = 512
N_BANK = 512
T_PASSES = T // K_PASS
V_PASSES = DV // K_PASS
DK_TILES = DK // P
TOK_TILES = T // P

I_TOK = 4
BLOCK = P * I_TOK
BLOCKS = T // BLOCK


def tile_linear_attention_state_backward_e2_kernel(
    tc, g_words, g_scales, h_words, h_scales, qg, state, gate, dq_rest, decay, ds_next, dq_out, ds_out
):
    nc = tc.nc
    with ExitStack() as ctx:
        keep = ctx.enter_context(tc.tile_pool(name="keep", bufs=1))
        outs = ctx.enter_context(tc.tile_pool(name="outs", bufs=4))
        psum = ctx.enter_context(tc.psum_pool(name="psum", bufs=4))
        ctx.enter_context(tc.manual_schedule())

        ident = keep.tile([P, P], F32, name="ident")
        make_identity(nc, ident[:])

        g_sc = keep.tile([P, T_PASSES, DV], U8, align_bytes=64, name="g_sc")
        h_sc = keep.tile([P, V_PASSES, T], U8, align_bytes=64, name="h_sc")
        nc.vector.memset(h_sc[:].rearrange("p g n -> p (g n)").bitcast(I32), 0)
        nc.vector.memset(g_sc[:].rearrange("p g n -> p (g n)").bitcast(I32), 0)

        def load_scales(tile, hbm):
            rows = hbm.rearrange("g (q r) n -> r q g n", r=4).bitcast(I32)
            for r in range(4):
                nc.sync.dma_start(out=tile[r : P : 32, :, :].bitcast(I32), in_=rows[r])


        st_raw = keep.tile([P, 4, DV], BF16, name="st_raw")
        st_view = state.rearrange("(r i) v -> r i v", i=4)

        def load_state(a):
            nc.sync.dma_start(out=st_raw[:, 2 * a : 2 * a + 2, :], in_=st_view[:, 2 * a : 2 * a + 2, :])

        h_w = [keep.tile([P, V_PASSES, T // 2], U32, align_bytes=64, name="h_w%d" % b) for b in range(2)]
        h_view = h_words.rearrange("g p n t -> p g (n t)").bitcast(I32)

        def load_h(b):
            nc.sync.dma_start(
                out=h_w[b][:].bitcast(I32), in_=h_view[:, :, b * (T // 2) : (b + 1) * (T // 2)]
            )

        gate_t = [keep.tile([P, I_TOK, DK], BF16, name="gate%d" % b) for b in range(BLOCKS)]
        rest_t = [keep.tile([P, I_TOK, DK], BF16, name="rest%d" % b) for b in range(BLOCKS)]
        gate_view = gate.rearrange("(b m i) k -> b m i k", m=P, i=I_TOK)
        rest_view = dq_rest.rearrange("(b m i) k -> b m i k", m=P, i=I_TOK)
        dq_view = dq_out.rearrange("(b m i) k -> b m i k", m=P, i=I_TOK)

        qg_raw = [keep.tile([P, 4, DK], BF16, name="qg_raw%d" % c) for c in range(T_PASSES)]

        def load_qg(c):
            nc.sync.dma_start(
                out=qg_raw[c][:],
                in_=qg[c * K_PASS : (c + 1) * K_PASS, :].rearrange("(p j) w -> p j w", j=4),
            )

        g_w = [keep.tile([P, DV], U32, align_bytes=64, name="g_w%d" % c) for c in range(T_PASSES)]

        def load_g(c):
            nc.sync.dma_start(
                out=g_w[c][:].bitcast(I32), in_=g_words[c].rearrange("p n t -> p (n t)").bitcast(I32)
            )

        dsn = keep.tile([P, DK_TILES, DV], BF16, name="dsn")

        def load_gate(b):
            nc.sync.dma_start(out=gate_t[b][:], in_=gate_view[b])

        def load_rest(b):
            nc.sync.dma_start(out=rest_t[b][:], in_=rest_view[b])

        dec_b = keep.tile([P, DK_TILES], BF16, name="dec_b")

        load_state(0)
        load_state(1)
        load_scales(h_sc, h_scales)
        load_h(0)
        load_gate(0)
        load_qg(0)
        load_rest(0)
        load_qg(1)
        load_gate(1)
        load_qg(2)
        load_rest(1)
        load_qg(3)
        load_scales(g_sc, g_scales)
        nc.sync.dma_start(out=dec_b[:], in_=decay.rearrange("(m t) -> m t", t=DK_TILES))
        for c in range(T_PASSES):
            load_g(c)
        load_h(1)
        nc.sync.dma_start(out=dsn[:], in_=ds_next.rearrange("(m t) v -> m t v", t=DK_TILES))
        load_gate(2)
        load_rest(2)
        load_gate(3)
        load_rest(3)

        qg_grp = [keep.tile([P, DK, 4], BF16, align_bytes=64, name="qg_grp%d" % c) for c in range(T_PASSES)]
        qg_c = [keep.tile([P, DK], U32, align_bytes=64, name="qg_c%d" % c) for c in range(T_PASSES)]
        qg_s = [keep.tile([P, DK], U8, align_bytes=64, name="qg_s%d" % c) for c in range(T_PASSES)]
        st_grp = [keep.tile([P, DK, 4], BF16, align_bytes=64, name="st_grp%d" % c) for c in range(V_PASSES)]
        st_c = [keep.tile([P, DK], U32, align_bytes=64, name="st_c%d" % c) for c in range(V_PASSES)]
        st_s = [keep.tile([P, DK], U8, align_bytes=64, name="st_s%d" % c) for c in range(V_PASSES)]

        def quantize(codes, scales, grouped):
            nc.vector.quantize_mx(
                out=codes[:].bitcast(E4M3X4), scales=scales[:], in_=grouped[:].rearrange("p w j -> p (w j)")
            )

        words = st_raw[:].rearrange("p i v -> p (i v)").bitcast(F32)

        def transpose_state(c, half):
            bank = psum.tile([P, 2, 2, P], F32, name="bank", tag="bank")
            for i in range(2):
                for u in range(2):
                    w0 = (2 * half + i) * (DV // 2) + c * (K_PASS // 2) + u
                    nc.tensor.transpose(bank[:, u, i, :], words[:, w0 : w0 + 2 * P - 1 : 2], ident[:])
            dst = st_grp[c][:].rearrange("p w t -> p (w t)").bitcast(F32)
            dst = dst.rearrange("p (r i u) -> p r i u", i=4, u=2)[:, :, 2 * half : 2 * half + 2, :]
            nc.scalar.copy(out=dst, in_=bank[:].rearrange("p u i r -> p r i u"))

        for half in range(2):
            for c in range(V_PASSES):
                transpose_state(c, half)
        for c in range(V_PASSES):
            quantize(st_c[c], st_s[c], st_grp[c])

        h_p = [keep.tile([P, V_PASSES, BLOCK], U32, align_bytes=64, name="h_p%d" % b) for b in range(BLOCKS)]
        h_ps = [keep.tile([P, V_PASSES, BLOCK], U8, align_bytes=64, name="h_ps%d" % b) for b in range(BLOCKS)]

        def permute(b):
            half, r = divmod(b * BLOCK, T // 2)
            for c in range(V_PASSES):
                nc.vector.tensor_copy(
                    out=h_p[b][:, c, :].bitcast(I32).rearrange("p (i mb mi) -> p mb i mi", i=I_TOK, mi=4),
                    in_=h_w[half][:, c, r : r + BLOCK].bitcast(I32).rearrange("p (mb mi i) -> p mb i mi", i=I_TOK, mi=4),
                )
                nc.vector.tensor_copy(
                    out=h_ps[b][:, c, :].rearrange("p (i mb mi) -> p mb i mi", i=I_TOK, mi=16),
                    in_=h_sc[:, c, b * BLOCK : (b + 1) * BLOCK].rearrange("p (mb mi i) -> p mb i mi", i=I_TOK, mi=16),
                )

        pending = []

        dq_sb = [keep.tile([P, I_TOK, DK], F32, name="dq_sb%d" % b) for b in range(BLOCKS)]

        def finish_pair():
            b, a, prod = pending.pop(0)
            toks = slice(2 * a, 2 * a + 2)
            eng = nc.vector if b < 2 else nc.gpsimd
            eng.tensor_tensor(out=dq_sb[b][:, toks, :], in0=prod[:], in1=rest_t[b][:, toks, :], op=ADD)
            if b == BLOCKS - 1:
                nc.sync.dma_start(out=dq_view[b, :, toks, :], in_=dq_sb[b][:, toks, :])
            elif a == 1:
                nc.sync.dma_start(out=dq_view[b], in_=dq_sb[b][:])

        banks = {}

        def queries_matmul(b, i):
            bank = psum.tile([P, DK], F32, name="bank", tag="bank")
            for c in range(V_PASSES):
                nc.tensor.matmul_mx(
                    out=bank[:],
                    lhsT=h_p[b][:, c, i * P : (i + 1) * P].bitcast(E5M2X4),
                    lhsT_scale=h_ps[b][:, c, i * P : (i + 1) * P],
                    rhs=st_c[c][:].bitcast(E4M3X4),
                    rhs_scale=st_s[c][:],
                    start=(c == 0),
                    stop=(c == V_PASSES - 1),
                )
            banks[b, i] = bank

        def queries_gate(b, a):
            prod = outs.tile([P, 2, DK], F32, name="prod")
            for j in range(2):
                i = 2 * a + j
                nc.vector.tensor_tensor(out=prod[:, j, :], in0=banks[b, i][:], in1=gate_t[b][:, i, :], op=MULT)
            if pending:
                finish_pair()
            pending.append((b, a, prod))

        def queries_block(b):
            for a in range(2):
                for j in range(2):
                    queries_matmul(b, 2 * a + j)
                queries_gate(b, a)

        acc = {}
        ds_view = ds_out.rearrange("(m t) v -> m t v", t=DK_TILES)

        def state_pass(a, c):
            for t in (2 * a, 2 * a + 1):
                for h in range(2):
                    if c == 0:
                        acc[t, h] = psum.tile([P, N_BANK], F32, name="acc", tag="acc")
                    ms = slice(t * P, (t + 1) * P)
                    ns = slice(h * N_BANK, (h + 1) * N_BANK)
                    nc.tensor.matmul_mx(
                        out=acc[t, h][:],
                        lhsT=qg_c[c][:, ms].bitcast(E4M3X4),
                        lhsT_scale=qg_s[c][:, ms],
                        rhs=g_w[c][:, ns].bitcast(E5M2X4),
                        rhs_scale=g_sc[:, c, ns],
                        start=(c == 0),
                        stop=(c == T_PASSES - 1),
                    )

        def state_finish(a):
            ds_sb = keep.tile([P, 2, DV], F32, name="ds_sb%d" % a)
            for t in (2 * a, 2 * a + 1):
                for h in range(2):
                    ns = slice(h * N_BANK, (h + 1) * N_BANK)
                    nc.vector.scalar_tensor_tensor(
                        out=ds_sb[:, t - 2 * a, ns],
                        in0=dsn[:, t, ns],
                        scalar=dec[:, t : t + 1],
                        in1=acc[t, h][:],
                        op0=MULT,
                        op1=ADD,
                    )
            nc.scalar.dma_start(out=ds_view[:, 2 * a : 2 * a + 2, :], in_=ds_sb[:])

        for c in range(T_PASSES):
            nc.scalar.copy(
                out=qg_grp[c][:].rearrange("p (t m) j -> p m t j", t=DK_TILES),
                in_=qg_raw[c][:].rearrange("p j (m t) -> p m t j", t=DK_TILES),
            )
        dec = keep.tile([P, DK_TILES], F32, name="dec")
        nc.scalar.copy(out=dec[:], in_=dec_b[:])

        permute(0)
        permute(1)
        queries_block(0)
        queries_block(1)
        finish_pair()
        for c in range(T_PASSES):
            quantize(qg_c[c], qg_s[c], qg_grp[c])
        permute(2)
        permute(3)
        for c in range(T_PASSES):
            state_pass(0, c)
        state_finish(0)
        for i in range(I_TOK):
            queries_matmul(2, i)
        queries_gate(2, 0)
        queries_gate(2, 1)
        for i in range(I_TOK):
            state_pass(1, i)
            queries_matmul(3, i)
        queries_gate(3, 0)
        queries_gate(3, 1)
        finish_pair()
        state_finish(1)
